import numpy as np, ml_dtypes
CORES = [88,96,104,112,120,216,224,232,240,248]
N = 10
DEG, TK, TIMES = 3, 128, 2
MASK = [[2,9,0],[2,9,1],[2,9,0],[2,9,3],[2,9,4],[2,9,5],[2,9,6],[2,9,7],[2,9,8],[2,9,0]]
def setup_inputs(rng):
    return {"x": rng.standard_normal((N, 128, TK), dtype=np.float32).astype(ml_dtypes.bfloat16), "w": (rng.standard_normal((N, 128, DEG * 128), dtype=np.float32) / np.float32(np.sqrt(128 * DEG / 2))).astype(ml_dtypes.bfloat16)}
def setup_inputs_big(rng):
    d = setup_inputs(rng)
    for k in ("x",): d[k] = (d[k].astype(np.float32) * 1048576.0).astype(d[k].dtype)
    return d
def setup_inputs_small(rng):
    d = setup_inputs(rng)
    for k in ("x",): d[k] = (d[k].astype(np.float32) * (1 / 1048576.0)).astype(d[k].dtype)
    return d
def setup_inputs_apart(rng):
    d = setup_inputs(rng)
    f = (10.0 ** rng.permutation(np.linspace(-1.5, 1.5, N))).astype(np.float32).reshape(N, 1, 1)
    for k in ("x",): d[k] = (d[k].astype(np.float32) * f).astype(d[k].dtype)
    return d
def reference(x, w):
    X, W = x.astype(np.float64), w.astype(np.float64)
    h = list(X)
    for _ in range(TIMES):
        h = [np.maximum(sum(W[r][:, 128 * i:128 * i + 128].T @ h[j] for i, j in enumerate(MASK[r])), 0.0) for r in range(N)]
    return {"y": np.stack(h).astype(ml_dtypes.bfloat16)}

@@ -1,0 +1,195 @@
+from concourse.bass import DstId, RemoteDMATransfer
+from concourse.mybir import AluOpType
+
+K = 128
+
+SCRATCH = {
+    "hub": ("sbuf", [128, 8 * K], "bfloat16"),
+    "own": ("sbuf", [128, 4 * K], "bfloat16"),
+    "hh": ("sbuf", [128, 2 * K], "bfloat16"),
+    "h1": ("sbuf", [128, K], "bfloat16"),
+    "yb": ("sbuf", [128, K], "bfloat16"),
+    "zero": ("sbuf", [128, K], "float32"),
+    "p0": ("psum", [128, 512], "float32"),
+    "p1": ("psum", [128, 512], "float32"),
+    "p2": ("psum", [128, 512], "float32"),
+    "p3": ("psum", [128, 512], "float32"),
+}
+SEMAPHORES = ["ldx", "ldw", "zs", "arrA", "arrB", "arrC", "arrW", "fx", "fh", "snt",
+              "m0", "m1", "m2", "m3", "rl", "r2", "r3", "st"]
+
+
+def _count(mask):
+    return len([i for i in range(mask.bit_length()) if (mask >> i) & 1])
+
+
+def _plan(T, topo):
+    M = T.tables["MASK"]
+    cores = list(T.cores)
+    a, b = M[0][0], M[0][1]
+    c = M[a][2]
+    hubs = (a, b)
+    for r in range(len(cores)):
+        assert list(M[r][:2]) == [a, b] and M[r][2] == (c if r in hubs else r)
+    leaves = [r for r in range(len(cores)) if r not in hubs]
+    direct = [r for r in leaves if all(topo.may_write(cores[h], cores[r]) for h in hubs)]
+    other = [r for r in leaves if r not in direct]
+    near_a = lambda r: topo.host(cores[r]) != topo.host(cores[a])
+    direct, other = sorted(direct, key=near_a), sorted(other, key=near_a)
+    serve_hub = {a: direct[:len(direct) // 2], b: direct[len(direct) // 2:]}
+    serve_help = {a: other[:len(other) // 2], b: other[len(other) // 2:]}
+    world = range((max(topo.host(k) for k in cores) + 1) * topo.CORES_PER_HOST)
+    helper = {}
+    for h in hubs:
+        hc = cores[h]
+        helper[h] = [k for k in world
+                     if (topo.host(k), topo.chip(k), topo.die(k)) == (topo.host(hc), topo.chip(hc), topo.die(hc))
+                     and k not in cores and all(topo.may_write(k, cores[r]) for r in serve_help[h])][0]
+    return M, cores, a, b, c, serve_hub, serve_help, helper
+
+
+def rank_program(g, core, T, topo):
+    M, cores, a, b, c, serve_hub, serve_help, helper = _plan(T, topo)
+    hubs = (a, b)
+    rank = T.rank_of(core)
+    help_of = [h for h in hubs if helper[h] == core]
+    if rank is None and not help_of:
+        return
+    S = T.sem
+    deg = len(M[0])
+    arr = {a: S.arrA, b: S.arrB}
+    blk = {a: T.hub[:, 0:4 * K], b: T.hub[:, 4 * K:8 * K]}
+    xs = {a: T.hub[:, 3 * K:4 * K], b: T.hub[:, 4 * K:5 * K]}
+    wbase = {a: 0, b: 5 * K}
+    xx = T.hub[:, 3 * K:5 * K]
+    own_x, own_w = T.own[:, 3 * K:4 * K], T.own[:, 0:3 * K]
+    hs = {a: T.hh[:, 0:K], b: T.hh[:, K:2 * K]}
+
+    def far_mask(src, dests):
+        m = topo.mask(src, dests[0])
+        for d in dests:
+            m &= topo.mask(src, d)
+        return m
+
+    def hub_masks(h):
+        o = hubs[1 - hubs.index(h)]
+        off = far_mask(cores[h], [helper[o], cores[o]])
+        return off, topo.mask(cores[h], helper[h]) & ~off
+
+    sent = [0]
+
+    def transfer(src, dst, dests, sem, mask):
+        ids = []
+        for d in dests:
+            rid, pid = topo.addr(d, core)
+            ids.append(DstId(rid=rid, pnc=pid))
+        sent[0] += _count(mask)
+        return RemoteDMATransfer(dst_ids=ids, dma_engine_mask=mask, remote_sem=sem,
+                                 srcs=[src], dsts=[dst for _ in dests], alu_op=0)
+
+    def relu(out, psum, after, done):
+        g.vector.wait_ge(after, 1)
+        g.vector.tensor_tensor(out, psum, T.zero[:, :], AluOpType.max).then_inc(done, 1)
+
+    waited = []
+
+    def pe_wait(waits):
+        for k, (s, v) in waits:
+            if k not in waited:
+                waited.append(k)
+                g.tensor.wait_ge(s, v)
+
+    def group(psum, terms, done):
+        ins = None
+        for t, (lhsT, rhs, waits) in enumerate(terms):
+            pe_wait(waits)
+            ins = g.tensor.matmul(psum, lhsT, rhs, t == 0, t == len(terms) - 1)
+        ins.then_inc(done, 1)
+
+    def store():
+        g.sync.wait_ge(S.r3, 1)
+        g.sync.dma_start(T.y[:, :], T.yb[:, :]).then_inc(S.st, 16)
+        g.sync.wait_ge(S.st, 16)
+
+    g.vector.memset(T.zero[:, :], 0.0).then_inc(S.zs, 1)
+    g.vector.wait_ge(S.zs, 1)
+
+    sites = [helper[a], helper[b], cores[a], cores[b]]
+    n_c = _count(far_mask(cores[c], sites))
+    loaded = [("ldx", (S.ldx, 16)), ("ldw", (S.ldw, 16))]
+
+    if rank in hubs or help_of:
+        near = rank if rank in hubs else help_of[0]
+        far = hubs[1 - hubs.index(near)]
+        n_far = _count(hub_masks(far)[0])
+        if rank in hubs:
+            g.sync.dma_start(xs[near], T.x[:, :]).then_inc(S.ldx, 16)
+            g.scalar.dma_start(T.hub[:, wbase[near]:wbase[near] + 3 * K], T.w[:, :]).then_inc(S.ldw, 16)
+            have_near = loaded
+            mine = [cores[r] for r in serve_hub[near]]
+        else:
+            have_near = [("near", (arr[near], _count(hub_masks(near)[1])))]
+            mine = [cores[r] for r in serve_help[near]]
+
+        for _, (s, v) in have_near:
+            g.wait_ge(s, v)
+        if rank in hubs:
+            off, on = hub_masks(near)
+            g.remote_dma_fused([transfer(blk[near], blk[near], [helper[far], cores[far]], arr[near], off),
+                                transfer(blk[near], blk[near], [helper[near]], arr[near], on)], local_sem=S.snt)
+        g.wait_ge(arr[far], n_far)
+        g.remote_dma_fused([transfer(xx, xx, mine, S.fx, far_mask(core, mine))], local_sem=S.snt)
+        g.wait_ge(S.rl, 2)
+        g.remote_dma_fused([transfer(T.hh[:, :], T.hh[:, :], mine, S.fh, far_mask(core, mine))], local_sem=S.snt)
+
+        ps, ms = {a: T.p0[:, 0:K], b: T.p1[:, 0:K]}, {a: S.m0, b: S.m1}
+        rhs = {a: xs[a], b: xs[b], c: own_x}
+        here, done, cnt = [], [], {a: 0, b: 0}
+        for what, waits in ((near, have_near), (far, [("far", (arr[far], n_far))]), (c, [("xc", (S.arrC, n_c))])):
+            pe_wait(waits)
+            here.append(what)
+            for j in hubs:
+                for i, src in enumerate(M[j]):
+                    if (j, i) in done or j not in here or src not in here:
+                        continue
+                    done.append((j, i))
+                    cnt[j] += 1
+                    ins = g.tensor.matmul(ps[j], T.hub[:, wbase[j] + K * i:wbase[j] + K * (i + 1)], rhs[src],
+                                          cnt[j] == 1, cnt[j] == deg)
+                    if cnt[j] == deg:
+                        ins.then_inc(ms[j], 1)
+        for j in hubs:
+            relu(hs[j], ps[j], ms[j], S.rl)
+
+        if rank in hubs:
+            group(T.p2[:, 0:K], [(T.own[:, K * i:K * (i + 1)], rhs[src], [("wc", (S.arrW, n_c))])
+                                 for i, src in enumerate(M[c])], S.m2)
+            relu(T.h1[:, :], T.p2[:, 0:K], S.m2, S.r2)
+            terms = [(T.hub[:, wbase[near] + K * i:wbase[near] + K * (i + 1)], hs[src] if src in hubs else T.h1[:, :],
+                      [("rl", (S.rl, 2))] if src in hubs else [("r2", (S.r2, 1))]) for i, src in enumerate(M[near])]
+            group(T.p3[:, 0:K], terms, S.m3)
+            relu(T.yb[:, :], T.p3[:, 0:K], S.m3, S.r3)
+            store()
+    else:
+        g.sync.dma_start(own_x, T.x[:, :]).then_inc(S.ldx, 16)
+        g.scalar.dma_start(own_w, T.w[:, :]).then_inc(S.ldw, 16)
+        served = [(helper[h], serve_help[h]) for h in hubs] + [(cores[h], serve_hub[h]) for h in hubs]
+        n_in = [_count(far_mask(s, [cores[r] for r in rs])) for s, rs in served if rank in rs][0]
+        if rank == c:
+            g.wait_ge(S.ldx, 16)
+            g.remote_dma_fused([transfer(own_x, own_x, sites, S.arrC, far_mask(core, sites))], local_sem=S.snt)
+            g.wait_ge(S.ldw, 16)
+            g.remote_dma_fused([transfer(own_w, own_w, [cores[a], cores[b]], S.arrW, far_mask(core, sites))],
+                               local_sem=S.snt)
+        w = [T.own[:, K * i:K * (i + 1)] for i in range(deg)]
+        order = sorted(range(deg), key=lambda i: M[rank][i] in hubs)
+        group(T.p0[:, 0:K], [(w[i], xs[M[rank][i]], [("fx", (S.fx, n_in))]) if M[rank][i] in hubs else
+                             (w[i], own_x, loaded) for i in order], S.m0)
+        relu(T.h1[:, :], T.p0[:, 0:K], S.m0, S.r2)
+        group(T.p1[:, 0:K], [(w[i], hs[M[rank][i]], [("fh", (S.fh, n_in))]) if M[rank][i] in hubs else
+                             (w[i], T.h1[:, :], [("r2", (S.r2, 1))]) for i in order], S.m1)
+        relu(T.yb[:, :], T.p1[:, 0:K], S.m1, S.r3)
+        store()
+
+    if sent[0]:
+        g.wait_ge(S.snt, sent[0])

@@ -1,11 +1,12 @@
 from concourse.bass import DstId, RemoteDMATransfer
-from concourse.mybir import AluOpType
+from concourse.mybir import AluOpType, ActivationFunctionType
 
 K = 128
 
 SCRATCH = {
     "hub": ("sbuf", [128, 8 * K], "bfloat16"),
     "own": ("sbuf", [128, 4 * K], "bfloat16"),
+    "xe": ("sbuf", [128, K], "bfloat16"),
     "hh": ("sbuf", [128, 2 * K], "bfloat16"),
     "h1": ("sbuf", [128, K], "bfloat16"),
     "yb": ("sbuf", [128, K], "bfloat16"),
@@ -15,7 +16,7 @@ SCRATCH = {
     "p2": ("psum", [128, 512], "float32"),
     "p3": ("psum", [128, 512], "float32"),
 }
-SEMAPHORES = ["ldx", "ldw", "zs", "arrA", "arrB", "arrC", "arrW", "fx", "fh", "snt",
+SEMAPHORES = ["ldx", "ldw", "zs", "arrA", "arrB", "arrC", "arrV", "arrW", "arrX", "fxA", "fxB", "fh", "snt",
               "m0", "m1", "m2", "m3", "rl", "r2", "r3", "st"]
 
 
@@ -36,32 +37,45 @@ def _plan(T, topo):
     other = [r for r in leaves if r not in direct]
     near_a = lambda r: topo.host(cores[r]) != topo.host(cores[a])
     direct, other = sorted(direct, key=near_a), sorted(other, key=near_a)
-    serve_hub = {a: direct[:len(direct) // 2], b: direct[len(direct) // 2:]}
-    serve_help = {a: other[:len(other) // 2], b: other[len(other) // 2:]}
+    dir_of = {a: direct[:len(direct) // 2], b: direct[len(direct) // 2:]}
+    oth_of = {a: other[:len(other) // 2], b: other[len(other) // 2:]}
+    serve_hub = {h: dir_of[h][:1] for h in hubs}
+    serve_help = {h: oth_of[h] + dir_of[h][1:] for h in hubs}
     world = range((max(topo.host(k) for k in cores) + 1) * topo.CORES_PER_HOST)
-    helper = {}
+    can = lambda k, rs: all(topo.may_write(k, cores[r]) for r in rs)
+
+    def chipmates(k0):
+        return [k for k in world if (topo.host(k), topo.chip(k)) == (topo.host(k0), topo.chip(k0)) and k not in cores]
+
+    helper, xway = {}, {}
     for h in hubs:
         hc = cores[h]
-        helper[h] = [k for k in world
-                     if (topo.host(k), topo.chip(k), topo.die(k)) == (topo.host(hc), topo.chip(hc), topo.die(hc))
-                     and k not in cores and all(topo.may_write(k, cores[r]) for r in serve_help[h])][0]
-    return M, cores, a, b, c, serve_hub, serve_help, helper
+        o = hubs[1 - hubs.index(h)]
+        helper[h] = [k for k in chipmates(hc) if topo.die(k) == topo.die(hc) and can(k, leaves)][0]
+        far_die = [k for k in chipmates(hc) if topo.die(k) != topo.die(hc)]
+        job1, job2 = oth_of[o] + direct[:1], direct[1:]
+        rel1 = [k for k in far_die if can(k, job1)][0]
+        rel2 = [k for k in far_die if can(k, job2) and k != rel1 and not can(k, other)][0]
+        xway[h] = [(helper[h], oth_of[h]), (rel1, job1), (rel2, job2)]
+    wrel = [k for k in chipmates(cores[c]) if topo.die(k) != topo.die(cores[c]) and can(k, hubs)][0]
+    return M, cores, a, b, c, serve_hub, serve_help, helper, xway, wrel
 
 
 def rank_program(g, core, T, topo):
-    M, cores, a, b, c, serve_hub, serve_help, helper = _plan(T, topo)
+    M, cores, a, b, c, serve_hub, serve_help, helper, xway, wrel = _plan(T, topo)
     hubs = (a, b)
     rank = T.rank_of(core)
     help_of = [h for h in hubs if helper[h] == core]
-    if rank is None and not help_of:
+    pass_of = [(h, rs) for h in hubs for k, rs in xway[h] if k == core]
+    if rank is None and not pass_of and core != wrel:
         return
     S = T.sem
     deg = len(M[0])
     arr = {a: S.arrA, b: S.arrB}
+    fx = {a: S.fxA, b: S.fxB}
     blk = {a: T.hub[:, 0:4 * K], b: T.hub[:, 4 * K:8 * K]}
     xs = {a: T.hub[:, 3 * K:4 * K], b: T.hub[:, 4 * K:5 * K]}
     wbase = {a: 0, b: 5 * K}
-    xx = T.hub[:, 3 * K:5 * K]
     own_x, own_w = T.own[:, 3 * K:4 * K], T.own[:, 0:3 * K]
     hs = {a: T.hh[:, 0:K], b: T.hh[:, K:2 * K]}
 
@@ -74,8 +88,12 @@ def rank_program(g, core, T, topo):
     def hub_masks(h):
         o = hubs[1 - hubs.index(h)]
         off = far_mask(cores[h], [helper[o], cores[o]])
-        return off, topo.mask(cores[h], helper[h]) & ~off
+        return off, far_mask(cores[h], [k for k, _ in xway[h]]) & ~off
 
+    sites = [helper[a], helper[b], cores[a], cores[b]]
+    c_off = far_mask(cores[c], sites)
+    c_on = topo.mask(cores[c], wrel) & ~c_off
+    w_off = far_mask(wrel, [cores[a], cores[b]])
     sent = [0]
 
     def transfer(src, dst, dests, sem, mask):
@@ -86,6 +104,24 @@ def rank_program(g, core, T, topo):
         sent[0] += _count(mask)
         return RemoteDMATransfer(dst_ids=ids, dma_engine_mask=mask, remote_sem=sem,
                                  srcs=[src], dsts=[dst for _ in dests], alu_op=0)
+
+    def send(src, dst, dests, sem, mask):
+        g.remote_dma_fused([transfer(src, dst, dests, sem, mask)], local_sem=S.snt)
+
+    def pass_x():
+        h, rs = pass_of[0]
+        dests = [cores[r] for r in rs]
+        g.wait_ge(S.arrX, _count(hub_masks(h)[1]))
+        send(T.xe[:, :], xs[h], dests, fx[h], far_mask(core, dests))
+
+    if rank is None and not help_of:
+        if core == wrel:
+            g.wait_ge(S.arrV, _count(c_on))
+            send(own_w, own_w, [cores[a], cores[b]], S.arrW, w_off)
+        else:
+            pass_x()
+        g.wait_ge(S.snt, sent[0])
+        return
 
     def relu(out, psum, after, done):
         g.vector.wait_ge(after, 1)
@@ -114,8 +150,6 @@ def rank_program(g, core, T, topo):
     g.vector.memset(T.zero[:, :], 0.0).then_inc(S.zs, 1)
     g.vector.wait_ge(S.zs, 1)
 
-    sites = [helper[a], helper[b], cores[a], cores[b]]
-    n_c = _count(far_mask(cores[c], sites))
     loaded = [("ldx", (S.ldx, 16)), ("ldw", (S.ldw, 16))]
 
     if rank in hubs or help_of:
@@ -131,21 +165,23 @@ def rank_program(g, core, T, topo):
             have_near = [("near", (arr[near], _count(hub_masks(near)[1])))]
             mine = [cores[r] for r in serve_help[near]]
 
-        for _, (s, v) in have_near:
-            g.wait_ge(s, v)
         if rank in hubs:
             off, on = hub_masks(near)
-            g.remote_dma_fused([transfer(blk[near], blk[near], [helper[far], cores[far]], arr[near], off),
+            g.wait_ge(S.ldx, 16)
+            send(xs[near], T.xe[:, :], [k for k, _ in xway[near]], S.arrX, on)
+            g.wait_ge(S.ldw, 16)
+            g.remote_dma_fused([transfer(blk[near], blk[near], [helper[far]], arr[near], off),
                                 transfer(blk[near], blk[near], [helper[near]], arr[near], on)], local_sem=S.snt)
-        g.wait_ge(arr[far], n_far)
-        g.remote_dma_fused([transfer(xx, xx, mine, S.fx, far_mask(core, mine))], local_sem=S.snt)
+            send(blk[near], blk[near], [cores[far]], arr[near], off)
+        else:
+            pass_x()
         g.wait_ge(S.rl, 2)
-        g.remote_dma_fused([transfer(T.hh[:, :], T.hh[:, :], mine, S.fh, far_mask(core, mine))], local_sem=S.snt)
+        send(T.hh[:, :], T.hh[:, :], mine, S.fh, far_mask(core, mine))
 
         ps, ms = {a: T.p0[:, 0:K], b: T.p1[:, 0:K]}, {a: S.m0, b: S.m1}
         rhs = {a: xs[a], b: xs[b], c: own_x}
         here, done, cnt = [], [], {a: 0, b: 0}
-        for what, waits in ((near, have_near), (far, [("far", (arr[far], n_far))]), (c, [("xc", (S.arrC, n_c))])):
+        for what, waits in ((near, have_near), (far, [("far", (arr[far], n_far))]), (c, [("xc", (S.arrC, _count(c_off)))])):
             pe_wait(waits)
             here.append(what)
             for j in hubs:
@@ -158,11 +194,12 @@ def rank_program(g, core, T, topo):
                                           cnt[j] == 1, cnt[j] == deg)
                     if cnt[j] == deg:
                         ins.then_inc(ms[j], 1)
-        for j in hubs:
-            relu(hs[j], ps[j], ms[j], S.rl)
+        relu(hs[a], ps[a], ms[a], S.rl)
+        g.scalar.wait_ge(ms[b], 1)
+        g.scalar.activation(hs[b], ps[b], ActivationFunctionType.Relu).then_inc(S.rl, 1)
 
         if rank in hubs:
-            group(T.p2[:, 0:K], [(T.own[:, K * i:K * (i + 1)], rhs[src], [("wc", (S.arrW, n_c))])
+            group(T.p2[:, 0:K], [(T.own[:, K * i:K * (i + 1)], rhs[src], [("wc", (S.arrW, _count(w_off)))])
                                  for i, src in enumerate(M[c])], S.m2)
             relu(T.h1[:, :], T.p2[:, 0:K], S.m2, S.r2)
             terms = [(T.hub[:, wbase[near] + K * i:wbase[near] + K * (i + 1)], hs[src] if src in hubs else T.h1[:, :],
@@ -175,16 +212,17 @@ def rank_program(g, core, T, topo):
         g.scalar.dma_start(own_w, T.w[:, :]).then_inc(S.ldw, 16)
         served = [(helper[h], serve_help[h]) for h in hubs] + [(cores[h], serve_hub[h]) for h in hubs]
         n_in = [_count(far_mask(s, [cores[r] for r in rs])) for s, rs in served if rank in rs][0]
+        n_x = {h: [_count(far_mask(k, [cores[r] for r in rs])) for k, rs in xway[h] if rank in rs][0] for h in hubs}
         if rank == c:
             g.wait_ge(S.ldx, 16)
-            g.remote_dma_fused([transfer(own_x, own_x, sites, S.arrC, far_mask(core, sites))], local_sem=S.snt)
+            send(own_x, own_x, [helper[a], helper[b]], S.arrC, c_off)
+            send(own_x, own_x, [cores[a], cores[b]], S.arrC, c_off)
             g.wait_ge(S.ldw, 16)
-            g.remote_dma_fused([transfer(own_w, own_w, [cores[a], cores[b]], S.arrW, far_mask(core, sites))],
-                               local_sem=S.snt)
+            send(own_w, own_w, [wrel], S.arrV, c_on)
         w = [T.own[:, K * i:K * (i + 1)] for i in range(deg)]
         order = sorted(range(deg), key=lambda i: M[rank][i] in hubs)
-        group(T.p0[:, 0:K], [(w[i], xs[M[rank][i]], [("fx", (S.fx, n_in))]) if M[rank][i] in hubs else
-                             (w[i], own_x, loaded) for i in order], S.m0)
+        group(T.p0[:, 0:K], [(w[i], xs[M[rank][i]], [("fx%d" % M[rank][i], (fx[M[rank][i]], n_x[M[rank][i]]))])
+                             if M[rank][i] in hubs else (w[i], own_x, loaded) for i in order], S.m0)
         relu(T.h1[:, :], T.p0[:, 0:K], S.m0, S.r2)
         group(T.p1[:, 0:K], [(w[i], hs[M[rank][i]], [("fh", (S.fh, n_in))]) if M[rank][i] in hubs else
                              (w[i], T.h1[:, :], [("r2", (S.r2, 1))]) for i in order], S.m1)

@@ -1,23 +1,21 @@
 from concourse.bass import DstId, RemoteDMATransfer
-from concourse.mybir import AluOpType, ActivationFunctionType
+from concourse.mybir import AluOpType
 
 K = 128
 
 SCRATCH = {
-    "hub": ("sbuf", [128, 8 * K], "bfloat16"),
     "own": ("sbuf", [128, 4 * K], "bfloat16"),
-    "xe": ("sbuf", [128, K], "bfloat16"),
+    "xx": ("sbuf", [128, 2 * K], "bfloat16"),
     "hh": ("sbuf", [128, 2 * K], "bfloat16"),
+    "xc": ("sbuf", [128, K], "bfloat16"),
+    "hc": ("sbuf", [128, K], "bfloat16"),
     "h1": ("sbuf", [128, K], "bfloat16"),
     "yb": ("sbuf", [128, K], "bfloat16"),
     "zero": ("sbuf", [128, K], "float32"),
     "p0": ("psum", [128, 512], "float32"),
     "p1": ("psum", [128, 512], "float32"),
-    "p2": ("psum", [128, 512], "float32"),
-    "p3": ("psum", [128, 512], "float32"),
 }
-SEMAPHORES = ["ldx", "ldw", "zs", "arrA", "arrB", "arrC", "arrV", "arrW", "arrX", "fxA", "fxB", "fh", "snt",
-              "m0", "m1", "m2", "m3", "rl", "r2", "r3", "st"]
+SEMAPHORES = ["ldx", "ldw", "zs", "fxA", "fxB", "fhA", "fhB", "arrC", "arrH", "snt", "m0", "m1", "r2", "r3", "st"]
 
 
 def _count(mask):
@@ -35,49 +33,44 @@ def _plan(T, topo):
     leaves = [r for r in range(len(cores)) if r not in hubs]
     direct = [r for r in leaves if all(topo.may_write(cores[h], cores[r]) for h in hubs)]
     other = [r for r in leaves if r not in direct]
-    near_a = lambda r: topo.host(cores[r]) != topo.host(cores[a])
-    direct, other = sorted(direct, key=near_a), sorted(other, key=near_a)
-    dir_of = {a: direct[:len(direct) // 2], b: direct[len(direct) // 2:]}
-    oth_of = {a: other[:len(other) // 2], b: other[len(other) // 2:]}
-    serve_hub = {h: dir_of[h][:1] for h in hubs}
-    serve_help = {h: oth_of[h] + dir_of[h][1:] for h in hubs}
+    assert c in direct
+    rest = [r for r in direct if r != c]
+    half = len(other) // 2
     world = range((max(topo.host(k) for k in cores) + 1) * topo.CORES_PER_HOST)
     can = lambda k, rs: all(topo.may_write(k, cores[r]) for r in rs)
-
-    def chipmates(k0):
-        return [k for k in world if (topo.host(k), topo.chip(k)) == (topo.host(k0), topo.chip(k0)) and k not in cores]
-
-    helper, xway = {}, {}
-    for h in hubs:
+    fan = {}
+    for n, h in enumerate(hubs):
         hc = cores[h]
-        o = hubs[1 - hubs.index(h)]
-        helper[h] = [k for k in chipmates(hc) if topo.die(k) == topo.die(hc) and can(k, leaves)][0]
-        far_die = [k for k in chipmates(hc) if topo.die(k) != topo.die(hc)]
-        job1, job2 = oth_of[o] + direct[:1], direct[1:]
-        rel1 = [k for k in far_die if can(k, job1)][0]
-        rel2 = [k for k in far_die if can(k, job2) and k != rel1 and not can(k, other)][0]
-        xway[h] = [(helper[h], oth_of[h]), (rel1, job1), (rel2, job2)]
-    wrel = [k for k in chipmates(cores[c]) if topo.die(k) != topo.die(cores[c]) and can(k, hubs)][0]
-    return M, cores, a, b, c, serve_hub, serve_help, helper, xway, wrel
+        o = hubs[1 - n]
+        mates = [k for k in world if (topo.host(k), topo.chip(k)) == (topo.host(hc), topo.chip(hc)) and k not in cores]
+        same = [k for k in mates if topo.die(k) == topo.die(hc)]
+        cross = [k for k in mates if topo.die(k) != topo.die(hc)]
+        e1 = [k for k in same if can(k, other)][0]
+        e2 = [k for k in cross if can(k, other)][0]
+        od = [k for k in cross if not can(k, other) and can(k, rest)][0]
+        third = rest[0] if n == 0 else rest[-1]
+        first, second = (other[:half], other[half:]) if n == 0 else (other[half:], other[:half])
+        fan[h] = ([cores[o], cores[c], cores[third]],
+                  [(e1, [cores[r] for r in first]), (e2, [cores[r] for r in second]),
+                   (od, [cores[r] for r in rest if r != third])])
+    return M, cores, a, b, c, fan
 
 
 def rank_program(g, core, T, topo):
-    M, cores, a, b, c, serve_hub, serve_help, helper, xway, wrel = _plan(T, topo)
+    M, cores, a, b, c, fan = _plan(T, topo)
     hubs = (a, b)
     rank = T.rank_of(core)
-    help_of = [h for h in hubs if helper[h] == core]
-    pass_of = [(h, rs) for h in hubs for k, rs in xway[h] if k == core]
-    if rank is None and not pass_of and core != wrel:
+    relay_of = [(h, ds) for h in hubs for k, ds in fan[h][1] if k == core]
+    if rank is None and not relay_of:
         return
     S = T.sem
     deg = len(M[0])
-    arr = {a: S.arrA, b: S.arrB}
     fx = {a: S.fxA, b: S.fxB}
-    blk = {a: T.hub[:, 0:4 * K], b: T.hub[:, 4 * K:8 * K]}
-    xs = {a: T.hub[:, 3 * K:4 * K], b: T.hub[:, 4 * K:5 * K]}
-    wbase = {a: 0, b: 5 * K}
-    own_x, own_w = T.own[:, 3 * K:4 * K], T.own[:, 0:3 * K]
+    fh = {a: S.fhA, b: S.fhB}
+    xs = {a: T.xx[:, 0:K], b: T.xx[:, K:2 * K]}
     hs = {a: T.hh[:, 0:K], b: T.hh[:, K:2 * K]}
+    own_x, own_w = T.own[:, 3 * K:4 * K], T.own[:, 0:3 * K]
+    w = [T.own[:, K * i:K * (i + 1)] for i in range(deg)]
 
     def far_mask(src, dests):
         m = topo.mask(src, dests[0])
@@ -86,14 +79,17 @@ def rank_program(g, core, T, topo):
         return m
 
     def hub_masks(h):
-        o = hubs[1 - hubs.index(h)]
-        off = far_mask(cores[h], [helper[o], cores[o]])
-        return off, far_mask(cores[h], [k for k, _ in xway[h]]) & ~off
+        off = far_mask(cores[h], fan[h][0])
+        full = far_mask(cores[h], [k for k, _ in fan[h][1]])
+        return off, full, full & ~off
 
-    sites = [helper[a], helper[b], cores[a], cores[b]]
-    c_off = far_mask(cores[c], sites)
-    c_on = topo.mask(cores[c], wrel) & ~c_off
-    w_off = far_mask(wrel, [cores[a], cores[b]])
+    def n_in(h, k):
+        if k in fan[h][0]:
+            return _count(hub_masks(h)[0])
+        return [_count(far_mask(rc, ds)) for rc, ds in fan[h][1] if k in ds][0]
+
+    hub_cores = [cores[a], cores[b]]
+    c_off = far_mask(cores[c], hub_cores)
     sent = [0]
 
     def transfer(src, dst, dests, sem, mask):
@@ -108,18 +104,14 @@ def rank_program(g, core, T, topo):
     def send(src, dst, dests, sem, mask):
         g.remote_dma_fused([transfer(src, dst, dests, sem, mask)], local_sem=S.snt)
 
-    def pass_x():
-        h, rs = pass_of[0]
-        dests = [cores[r] for r in rs]
-        g.wait_ge(S.arrX, _count(hub_masks(h)[1]))
-        send(T.xe[:, :], xs[h], dests, fx[h], far_mask(core, dests))
-
-    if rank is None and not help_of:
-        if core == wrel:
-            g.wait_ge(S.arrV, _count(c_on))
-            send(own_w, own_w, [cores[a], cores[b]], S.arrW, w_off)
-        else:
-            pass_x()
+    if rank is None:
+        h, ds = relay_of[0]
+        _, full, on = hub_masks(h)
+        m = far_mask(core, ds)
+        g.wait_ge(fx[h], _count(on))
+        send(xs[h], xs[h], ds, fx[h], m)
+        g.wait_ge(fh[h], _count(full))
+        send(hs[h], hs[h], ds, fh[h], m)
         g.wait_ge(S.snt, sent[0])
         return
 
@@ -129,105 +121,58 @@ def rank_program(g, core, T, topo):
 
     waited = []
 
-    def pe_wait(waits):
-        for k, (s, v) in waits:
-            if k not in waited:
-                waited.append(k)
-                g.tensor.wait_ge(s, v)
-
     def group(psum, terms, done):
         ins = None
         for t, (lhsT, rhs, waits) in enumerate(terms):
-            pe_wait(waits)
+            for k, (s, v) in waits:
+                if k not in waited:
+                    waited.append(k)
+                    g.tensor.wait_ge(s, v)
             ins = g.tensor.matmul(psum, lhsT, rhs, t == 0, t == len(terms) - 1)
         ins.then_inc(done, 1)
 
-    def store():
-        g.sync.wait_ge(S.r3, 1)
-        g.sync.dma_start(T.y[:, :], T.yb[:, :]).then_inc(S.st, 16)
-        g.sync.wait_ge(S.st, 16)
-
     g.vector.memset(T.zero[:, :], 0.0).then_inc(S.zs, 1)
     g.vector.wait_ge(S.zs, 1)
-
     loaded = [("ldx", (S.ldx, 16)), ("ldw", (S.ldw, 16))]
+    is_hub = rank in hubs
+    my_x = xs[rank] if is_hub else own_x
+    my_h = hs[rank] if is_hub else T.h1[:, :]
+    g.sync.dma_start(my_x, T.x[:, :]).then_inc(S.ldx, 16)
+    g.scalar.dma_start(own_w, T.w[:, :]).then_inc(S.ldw, 16)
 
-    if rank in hubs or help_of:
-        near = rank if rank in hubs else help_of[0]
-        far = hubs[1 - hubs.index(near)]
-        n_far = _count(hub_masks(far)[0])
-        if rank in hubs:
-            g.sync.dma_start(xs[near], T.x[:, :]).then_inc(S.ldx, 16)
-            g.scalar.dma_start(T.hub[:, wbase[near]:wbase[near] + 3 * K], T.w[:, :]).then_inc(S.ldw, 16)
-            have_near = loaded
-            mine = [cores[r] for r in serve_hub[near]]
-        else:
-            have_near = [("near", (arr[near], _count(hub_masks(near)[1])))]
-            mine = [cores[r] for r in serve_help[near]]
+    if is_hub:
+        off, full, on = hub_masks(rank)
+        mine, relays = fan[rank][0], [k for k, _ in fan[rank][1]]
+        g.wait_ge(S.ldx, 16)
+        g.remote_dma_fused([transfer(my_x, my_x, mine, fx[rank], off),
+                            transfer(my_x, my_x, relays, fx[rank], on)], local_sem=S.snt)
+        g.wait_ge(S.r2, 1)
+        send(my_h, my_h, relays, fh[rank], full)
+        send(my_h, my_h, mine, fh[rank], off)
+    elif rank == c:
+        g.wait_ge(S.ldx, 16)
+        send(own_x, T.xc[:, :], hub_cores, S.arrC, c_off)
+        g.wait_ge(S.r2, 1)
+        send(my_h, T.hc[:, :], hub_cores, S.arrH, c_off)
 
-        if rank in hubs:
-            off, on = hub_masks(near)
-            g.wait_ge(S.ldx, 16)
-            send(xs[near], T.xe[:, :], [k for k, _ in xway[near]], S.arrX, on)
-            g.wait_ge(S.ldw, 16)
-            g.remote_dma_fused([transfer(blk[near], blk[near], [helper[far]], arr[near], off),
-                                transfer(blk[near], blk[near], [helper[near]], arr[near], on)], local_sem=S.snt)
-            send(blk[near], blk[near], [cores[far]], arr[near], off)
-        else:
-            pass_x()
-        g.wait_ge(S.rl, 2)
-        send(T.hh[:, :], T.hh[:, :], mine, S.fh, far_mask(core, mine))
+    def term(i, second):
+        src = M[rank][i]
+        if src == rank:
+            return (w[i], my_h, [("r2", (S.r2, 1))]) if second else (w[i], my_x, loaded)
+        if src in hubs:
+            n = n_in(src, core)
+            return (w[i], hs[src], [("fh%d" % src, (fh[src], n))]) if second else (w[i], xs[src], [("fx%d" % src, (fx[src], n))])
+        n = _count(c_off)
+        return (w[i], T.hc[:, :], [("hc", (S.arrH, n))]) if second else (w[i], T.xc[:, :], [("xc", (S.arrC, n))])
 
-        ps, ms = {a: T.p0[:, 0:K], b: T.p1[:, 0:K]}, {a: S.m0, b: S.m1}
-        rhs = {a: xs[a], b: xs[b], c: own_x}
-        here, done, cnt = [], [], {a: 0, b: 0}
-        for what, waits in ((near, have_near), (far, [("far", (arr[far], n_far))]), (c, [("xc", (S.arrC, _count(c_off)))])):
-            pe_wait(waits)
-            here.append(what)
-            for j in hubs:
-                for i, src in enumerate(M[j]):
-                    if (j, i) in done or j not in here or src not in here:
-                        continue
-                    done.append((j, i))
-                    cnt[j] += 1
-                    ins = g.tensor.matmul(ps[j], T.hub[:, wbase[j] + K * i:wbase[j] + K * (i + 1)], rhs[src],
-                                          cnt[j] == 1, cnt[j] == deg)
-                    if cnt[j] == deg:
-                        ins.then_inc(ms[j], 1)
-        relu(hs[a], ps[a], ms[a], S.rl)
-        g.scalar.wait_ge(ms[b], 1)
-        g.scalar.activation(hs[b], ps[b], ActivationFunctionType.Relu).then_inc(S.rl, 1)
-
-        if rank in hubs:
-            group(T.p2[:, 0:K], [(T.own[:, K * i:K * (i + 1)], rhs[src], [("wc", (S.arrW, _count(w_off)))])
-                                 for i, src in enumerate(M[c])], S.m2)
-            relu(T.h1[:, :], T.p2[:, 0:K], S.m2, S.r2)
-            terms = [(T.hub[:, wbase[near] + K * i:wbase[near] + K * (i + 1)], hs[src] if src in hubs else T.h1[:, :],
-                      [("rl", (S.rl, 2))] if src in hubs else [("r2", (S.r2, 1))]) for i, src in enumerate(M[near])]
-            group(T.p3[:, 0:K], terms, S.m3)
-            relu(T.yb[:, :], T.p3[:, 0:K], S.m3, S.r3)
-            store()
-    else:
-        g.sync.dma_start(own_x, T.x[:, :]).then_inc(S.ldx, 16)
-        g.scalar.dma_start(own_w, T.w[:, :]).then_inc(S.ldw, 16)
-        served = [(helper[h], serve_help[h]) for h in hubs] + [(cores[h], serve_hub[h]) for h in hubs]
-        n_in = [_count(far_mask(s, [cores[r] for r in rs])) for s, rs in served if rank in rs][0]
-        n_x = {h: [_count(far_mask(k, [cores[r] for r in rs])) for k, rs in xway[h] if rank in rs][0] for h in hubs}
-        if rank == c:
-            g.wait_ge(S.ldx, 16)
-            send(own_x, own_x, [helper[a], helper[b]], S.arrC, c_off)
-            send(own_x, own_x, [cores[a], cores[b]], S.arrC, c_off)
-            g.wait_ge(S.ldw, 16)
-            send(own_w, own_w, [wrel], S.arrV, c_on)
-        w = [T.own[:, K * i:K * (i + 1)] for i in range(deg)]
-        order = sorted(range(deg), key=lambda i: M[rank][i] in hubs)
-        group(T.p0[:, 0:K], [(w[i], xs[M[rank][i]], [("fx%d" % M[rank][i], (fx[M[rank][i]], n_x[M[rank][i]]))])
-                             if M[rank][i] in hubs else (w[i], own_x, loaded) for i in order], S.m0)
-        relu(T.h1[:, :], T.p0[:, 0:K], S.m0, S.r2)
-        group(T.p1[:, 0:K], [(w[i], hs[M[rank][i]], [("fh", (S.fh, n_in))]) if M[rank][i] in hubs else
-                             (w[i], T.h1[:, :], [("r2", (S.r2, 1))]) for i in order], S.m1)
-        relu(T.yb[:, :], T.p1[:, 0:K], S.m1, S.r3)
-        store()
+    order = sorted(range(deg), key=lambda i: (M[rank][i] != rank, M[rank][i] not in hubs))
+    group(T.p0[:, 0:K], [term(i, False) for i in order], S.m0)
+    relu(my_h, T.p0[:, 0:K], S.m0, S.r2)
+    group(T.p1[:, 0:K], [term(i, True) for i in order], S.m1)
+    relu(T.yb[:, :], T.p1[:, 0:K], S.m1, S.r3)
+    g.sync.wait_ge(S.r3, 1)
+    g.sync.dma_start(T.y[:, :], T.yb[:, :]).then_inc(S.st, 16)
+    g.sync.wait_ge(S.st, 16)
 
     if sent[0]:
         g.wait_ge(S.snt, sent[0])

from concourse.bass import DstId, RemoteDMATransfer
from concourse.mybir import AluOpType

K = 128

SCRATCH = {
    "own": ("sbuf", [128, 4 * K], "bfloat16"),
    "xx": ("sbuf", [128, 2 * K], "bfloat16"),
    "hh": ("sbuf", [128, 2 * K], "bfloat16"),
    "xc": ("sbuf", [128, K], "bfloat16"),
    "hc": ("sbuf", [128, K], "bfloat16"),
    "h1": ("sbuf", [128, K], "bfloat16"),
    "yb": ("sbuf", [128, K], "bfloat16"),
    "zero": ("sbuf", [128, K], "float32"),
    "p0": ("psum", [128, 512], "float32"),
    "p1": ("psum", [128, 512], "float32"),
}
SEMAPHORES = ["ldx", "ldw", "zs", "fxA", "fxB", "fhA", "fhB", "arrC", "arrH", "snt", "m0", "m1", "r2", "r3", "st"]


def _count(mask):
    return len([i for i in range(mask.bit_length()) if (mask >> i) & 1])


def _plan(T, topo):
    M = T.tables["MASK"]
    cores = list(T.cores)
    a, b = M[0][0], M[0][1]
    c = M[a][2]
    hubs = (a, b)
    for r in range(len(cores)):
        assert list(M[r][:2]) == [a, b] and M[r][2] == (c if r in hubs else r)
    leaves = [r for r in range(len(cores)) if r not in hubs]
    direct = [r for r in leaves if all(topo.may_write(cores[h], cores[r]) for h in hubs)]
    other = [r for r in leaves if r not in direct]
    assert c in direct
    rest = [r for r in direct if r != c]
    half = len(other) // 2
    world = range((max(topo.host(k) for k in cores) + 1) * topo.CORES_PER_HOST)
    can = lambda k, rs: all(topo.may_write(k, cores[r]) for r in rs)
    fan = {}
    for n, h in enumerate(hubs):
        hc = cores[h]
        o = hubs[1 - n]
        mates = [k for k in world if (topo.host(k), topo.chip(k)) == (topo.host(hc), topo.chip(hc)) and k not in cores]
        same = [k for k in mates if topo.die(k) == topo.die(hc)]
        cross = [k for k in mates if topo.die(k) != topo.die(hc)]
        e1 = [k for k in same if can(k, other)][0]
        e2 = [k for k in cross if can(k, other)][0]
        od = [k for k in cross if not can(k, other) and can(k, rest)][0]
        third = rest[0] if n == 0 else rest[-1]
        first, second = (other[:half], other[half:]) if n == 0 else (other[half:], other[:half])
        fan[h] = ([cores[o], cores[c], cores[third]],
                  [(e1, [cores[r] for r in first]), (e2, [cores[r] for r in second]),
                   (od, [cores[r] for r in rest if r != third])])
    return M, cores, a, b, c, fan


def rank_program(g, core, T, topo):
    M, cores, a, b, c, fan = _plan(T, topo)
    hubs = (a, b)
    rank = T.rank_of(core)
    relay_of = [(h, ds) for h in hubs for k, ds in fan[h][1] if k == core]
    if rank is None and not relay_of:
        return
    S = T.sem
    deg = len(M[0])
    fx = {a: S.fxA, b: S.fxB}
    fh = {a: S.fhA, b: S.fhB}
    xs = {a: T.xx[:, 0:K], b: T.xx[:, K:2 * K]}
    hs = {a: T.hh[:, 0:K], b: T.hh[:, K:2 * K]}
    own_x, own_w = T.own[:, 3 * K:4 * K], T.own[:, 0:3 * K]
    w = [T.own[:, K * i:K * (i + 1)] for i in range(deg)]

    def far_mask(src, dests):
        m = topo.mask(src, dests[0])
        for d in dests:
            m &= topo.mask(src, d)
        return m

    def hub_masks(h):
        off = far_mask(cores[h], fan[h][0])
        full = far_mask(cores[h], [k for k, _ in fan[h][1]])
        return off, full, full & ~off

    def n_in(h, k):
        if k in fan[h][0]:
            return _count(hub_masks(h)[0])
        return [_count(far_mask(rc, ds)) for rc, ds in fan[h][1] if k in ds][0]

    hub_cores = [cores[a], cores[b]]
    c_off = far_mask(cores[c], hub_cores)
    sent = [0]

    def transfer(src, dst, dests, sem, mask):
        ids = []
        for d in dests:
            rid, pid = topo.addr(d, core)
            ids.append(DstId(rid=rid, pnc=pid))
        sent[0] += _count(mask)
        return RemoteDMATransfer(dst_ids=ids, dma_engine_mask=mask, remote_sem=sem,
                                 srcs=[src], dsts=[dst for _ in dests], alu_op=0)

    def send(src, dst, dests, sem, mask):
        g.remote_dma_fused([transfer(src, dst, dests, sem, mask)], local_sem=S.snt)

    if rank is None:
        h, ds = relay_of[0]
        _, full, on = hub_masks(h)
        m = far_mask(core, ds)
        g.wait_ge(fx[h], _count(on))
        send(xs[h], xs[h], ds, fx[h], m)
        g.wait_ge(fh[h], _count(full))
        send(hs[h], hs[h], ds, fh[h], m)
        g.wait_ge(S.snt, sent[0])
        return

    def relu(out, psum, after, done):
        g.vector.wait_ge(after, 1)
        g.vector.tensor_tensor(out, psum, T.zero[:, :], AluOpType.max).then_inc(done, 1)

    waited = []

    def group(psum, terms, done):
        ins = None
        for t, (lhsT, rhs, waits) in enumerate(terms):
            for k, (s, v) in waits:
                if k not in waited:
                    waited.append(k)
                    g.tensor.wait_ge(s, v)
            ins = g.tensor.matmul(psum, lhsT, rhs, t == 0, t == len(terms) - 1)
        ins.then_inc(done, 1)

    g.vector.memset(T.zero[:, :], 0.0).then_inc(S.zs, 1)
    g.vector.wait_ge(S.zs, 1)
    loaded = [("ldx", (S.ldx, 16)), ("ldw", (S.ldw, 16))]
    is_hub = rank in hubs
    my_x = xs[rank] if is_hub else own_x
    my_h = hs[rank] if is_hub else T.h1[:, :]
    g.sync.dma_start(my_x, T.x[:, :]).then_inc(S.ldx, 16)
    g.scalar.dma_start(own_w, T.w[:, :]).then_inc(S.ldw, 16)

    if is_hub:
        off, full, on = hub_masks(rank)
        mine, relays = fan[rank][0], [k for k, _ in fan[rank][1]]
        g.wait_ge(S.ldx, 16)
        g.remote_dma_fused([transfer(my_x, my_x, mine, fx[rank], off),
                            transfer(my_x, my_x, relays, fx[rank], on)], local_sem=S.snt)
        g.wait_ge(S.r2, 1)
        send(my_h, my_h, relays, fh[rank], full)
        send(my_h, my_h, mine, fh[rank], off)
    elif rank == c:
        g.wait_ge(S.ldx, 16)
        send(own_x, T.xc[:, :], hub_cores, S.arrC, c_off)
        g.wait_ge(S.r2, 1)
        send(my_h, T.hc[:, :], hub_cores, S.arrH, c_off)

    def term(i, second):
        src = M[rank][i]
        if src == rank:
            return (w[i], my_h, [("r2", (S.r2, 1))]) if second else (w[i], my_x, loaded)
        if src in hubs:
            n = n_in(src, core)
            return (w[i], hs[src], [("fh%d" % src, (fh[src], n))]) if second else (w[i], xs[src], [("fx%d" % src, (fx[src], n))])
        n = _count(c_off)
        return (w[i], T.hc[:, :], [("hc", (S.arrH, n))]) if second else (w[i], T.xc[:, :], [("xc", (S.arrC, n))])

    order = sorted(range(deg), key=lambda i: (M[rank][i] != rank, M[rank][i] not in hubs))
    group(T.p0[:, 0:K], [term(i, False) for i in order], S.m0)
    relu(my_h, T.p0[:, 0:K], S.m0, S.r2)
    group(T.p1[:, 0:K], [term(i, True) for i in order], S.m1)
    relu(T.yb[:, :], T.p1[:, 0:K], S.m1, S.r3)
    g.sync.wait_ge(S.r3, 1)
    g.sync.dma_start(T.y[:, :], T.yb[:, :]).then_inc(S.st, 16)
    g.sync.wait_ge(S.st, 16)

    if sent[0]:
        g.wait_ge(S.snt, sent[0])
